import numpy as np, ml_dtypes
CORES = [24,25,26,27,28,29,30,31]
N = 8
BF = ml_dtypes.bfloat16
W, L, M, P, Q, F, RO = 2048, 8, 8, 16, 16, 4, 2
CAP = (N - 1) * Q
def look(u, m):
    return (u * (u >> 5) + (2 * m + 1) * u) & (W - 1)
def pick(x, ix):
    return np.take_along_axis(x, ix[..., None, :], -1)
def pack(x, w, th):
    return {"x0": np.ascontiguousarray(x.reshape(N, 128, W)).astype(np.float32).astype(BF), "wt": np.ascontiguousarray(w).reshape(N, 128, 1).astype(np.float32).astype(BF),
            "th": np.repeat(th, 16, axis=1).astype(np.int32)}
def texture(rng):
    x = np.empty((N, 8, 16, W), np.int64); stock = rng.permutation(np.array([8, 24, 60, 120, 200, 300, 400, 600]))
    for g in range(8):
        n = int(stock[g]); base = rng.integers(0, 256, (n, 16))
        for q in range(N):
            e = 1.5 + rng.random()
            x[q, g] = (base[np.minimum((n * rng.random(W) ** e).astype(np.int64), n - 1)] + rng.integers(-2, 3, (W, 16))).T
    return np.clip(x, 0, 255)
def far(rng):
    return rng.integers(0, 256, (N, 8, 16, W))
def weights(rng):
    w = rng.integers(0, 256, (8, 16)); w[:, 0] = 1; w[:, 1] = 16; w[:, 13:] = 0
    return w
def with_hash(rng, w, u):
    k = rng.integers(0, 256, (len(u), 16)); v = (u - k[:, 2:] @ w[2:]) & (W - 1)
    k[:, 0] = v & 15; k[:, 1] = v >> 4
    return k
def odd(rng, m, n):
    u = np.arange(1, W, 2); u = rng.permutation(u[((u >> 5) & 1) == 0])
    i = np.unique(look(u, m), return_index=True)[1]
    assert len(i) >= n
    return rng.permutation(u[i])[:n]
def runs(rng):
    r = W // (L + F); n = min(r, CAP + 12)
    return L * np.sort(rng.permutation(r)[:n]) + L - 2
def setup_inputs(rng):
    return pack(texture(rng), rng.integers(0, 256, (N, 8, 16)), rng.integers(20, 41, (N, 8, 2)))
def setup_inputs_room(rng):
    x = far(rng); w = weights(rng); th = np.stack([rng.integers(1, 60, (N, 8)), rng.choice(np.array([1, 2, 40]), (N, 8))], axis=-1)
    th[rng.integers(0, N), rng.integers(4, 6), 1] = 0
    for g in range(8):
        m = g % M; p = runs(rng); n = len(p); u = odd(rng, m, n); c = look(u, m); k = with_hash(rng, w[g], u)
        for q in range(N):
            a = int(rng.choice(np.array([0, 1, CAP - 1, CAP, CAP + 1, n])))
            if q == 0: a = (CAP, CAP + 1, n, CAP - 1, 1, 0, CAP, CAP + 1)[g]
            i = rng.permutation(n)[:a]
            x[q, g][:, c] = k.T; x[q, g][:, p[i]] = k[i].T
    return pack(x, np.broadcast_to(w, (N, 8, 16)), th)
def setup_inputs_ties(rng):
    x = far(rng); w = weights(rng); t = rng.integers(2, 250, 8); t2 = t + rng.integers(-1, 2, (N, 8))
    for g in range(1, 8, 2):
        a = 4 * int(rng.integers(65, 124)) + g % 4; t2[:, g] = a; t[g] = a + int(rng.integers(0, 2))
    th = np.stack([np.broadcast_to(t, (N, 8)), t2], axis=-1)
    for g in range(8):
        m = g % M; p = runs(rng); n = len(p); u = odd(rng, m, n); k = with_hash(rng, w[g], u); k[:, 13:] = 0; more = 255 * (g % 2)
        for q in range(N):
            for c in (look(u, m + 1), look(u, m)):
                z = k + 0; z[:, 14] = rng.integers(0, 3, n); x[q, g][:, c] = z.T
            z = k + 0; z[:, 13] = more; z[:, 15] = t[g] - more + rng.integers(-2, 1, n); x[q, g][:, p] = z.T
    return pack(x, np.broadcast_to(w, (N, 8, 16)), th)
def over_the_end(rng, x, w, g):
    p = W - L - 2; every = np.arange(W); first = look(every, 0); later = look(every, np.arange(1, P)[:, None])
    good = (first >= L) & (first < p - L)
    j, uk = np.nonzero((later > W - F) & good & ~np.any(later == p, axis=0))
    i = int(rng.integers(0, len(uk))); u = int(uk[i]); c1 = int(first[u]); c2 = int(later[j[i], u])
    a = int(rng.choice(every[good & (first != c1)])); ca = int(first[a])
    k = with_hash(rng, w[g], np.array([u]))[0]; k[15] = 0; near = k + 0; near[15] = 3
    ka = with_hash(rng, w[g], np.full(N, a))
    for q in range(N):
        x[q, g][:, [0, ca]] = ka[q][:, None]; x[q, g][:, c1] = near; x[q, g][:, [p, c2 - F]] = k[:, None]
def setup_inputs_ends(rng):
    x = far(rng); w = weights(rng); th = rng.integers(1, 60, (N, 8, 2))
    mm, uu = np.nonzero(look(np.arange(W), np.arange(M)[:, None]) >= W - L // 2)
    for g in range(8):
        if g % 4 == 3:
            over_the_end(rng, x, w, g); th[:, g] = rng.integers(4, 60, (N, 2))
            continue
        if g % 2 == 0:
            o = rng.permutation(len(uu)); c, i = np.unique(look(uu[o], mm[o]), return_index=True); u = uu[o][i]; p = L * rng.permutation(len(u))
        else:
            u = odd(rng, g % M, 1); c = look(u, g % M); p = np.array([W - 2])
        k = with_hash(rng, w[g], u)
        for q in range(N):
            x[q, g][:, c] = k.T; x[q, g][:, p] = k.T
    return pack(x, np.broadcast_to(w, (N, 8, 16)), th)
def setup_inputs_alike(rng):
    x = texture(rng); w = rng.integers(0, 256, (N, 8, 16)); th = rng.integers(20, 41, (N, 8, 2))
    for g in range(0, 8, 2):
        base = rng.integers(0, 256, (4, 16)); x[:, g] = base[rng.integers(0, 4, (N, W))].transpose(0, 2, 1)
    th[:, 0] = 1; th[:, 2] = 4096; th[:, 4, 0] = 0; th[:, 1, 0] = 4096; th[:, 1, 1] = 0; th[:, 3, 1] = 4096
    w[:, 6] = 0; w[:, 5] = 255
    x[:, 1, :, 0] = 255
    w[:, 7] = rng.integers(230, 256, (N, 16))
    up = rng.random((N, 1, W)) < 0.5; up[::2] = False
    x[:, 7] = np.where(up, 255 - rng.integers(0, 40, (N, 16, W)), rng.integers(0, 40, (N, 16, W)))
    for q in range(N):
        x[q, 1][:, L * (1 + rng.permutation(W // L - 1)[:W // L // 2])] = 0
        if q % 2 == 0:
            th[q, 7, 0] = rng.integers(150, 260); th[q, 7, 1] = rng.integers(3100, 3600)
        else:
            th[q, 7, 0] = rng.integers(2048, 3000); th[q, 7, 1] = rng.integers(100, 4097)
            c = look((255 * int(np.sum(w[q, 7]))) & (W - 1), 0); x[q, 7][:, [0, L, c]] = 255
    th[0, 7, 1] = 4096
    return pack(x, w, th)
def setup_inputs_spread(rng):
    x = np.minimum((np.exp2(8 * rng.random((N, 8, 1, W))) * rng.random((N, 8, 16, W))).astype(np.int64), 255)
    w = np.minimum(np.exp2(8 * rng.random((N, 8, 16))).astype(np.int64), 255) * (rng.random((N, 8, 16)) > 0.0625)
    return pack(x, w, np.minimum(np.exp2(12 * rng.random((N, 8, 2))).astype(np.int64), 4096))
def check_inputs(d):
    bad = []
    for k in ("x0", "wt"):
        v = np.asarray(d[k]).astype(np.float32)
        if not np.all((v >= 0) & (v <= 255) & (v == np.floor(v))): bad.append("whole numbers of " + k)
    v = np.asarray(d["th"])
    if np.min(v) < 0 or np.max(v) > 4096: bad.append("range of th")
    v = v.reshape(N, 8, 16, 2)
    if np.any(v != v[:, :, :1]): bad.append("rows of th alike in a group")
    return bad
def reference(x0, wt, th):
    x = x0.astype(np.float32).astype(np.int64).reshape(N, 8, 16, W); w = wt.astype(np.float32).astype(np.int64).reshape(N, 8, 16, 1)
    t = th.astype(np.int64).reshape(N, 8, 16, 2)[:, :, 0]; here = np.arange(W)
    for rnd in range(RO):
        u = np.add.reduce(w * x, axis=2) & (W - 1)
        nx = np.zeros_like(u) + ((here + 1) & (W - 1))
        for m in range(M - 1, -1, -1):
            c = look(u, m); near = np.add.reduce(np.abs(pick(x, c) - x), axis=2) < t[..., :1]
            nx = np.where(near, (c + 1) & (W - 1), nx)
        s = np.zeros((N, 8, W // L, L), np.int64); s[..., 0] = L * np.arange(W // L)
        for k in range(1, L): s[..., k] = np.take_along_axis(nx, s[..., k - 1], -1)
        jump = np.zeros(s.shape, bool); jump[..., :-1] = s[..., 1:] != ((s[..., :-1] + 1) & (W - 1))
        s = s.reshape(N, 8, W); jump = jump.reshape(N, 8, W)
        site = np.argsort(~jump, axis=-1, kind="stable")[..., :CAP]
        live = np.take_along_axis(jump, site, -1); ask = pick(x, np.take_along_axis(s, site, -1))
        found = np.zeros((N, 8, CAP), bool); fill = np.zeros((N, 8, 16, CAP, F), np.int64)
        for q in range(N):
            for d in range(1, N):
                b = (q + d) % N; cut = slice((d - 1) * Q, d * Q); a = ask[q][:, :, cut]
                v = np.add.reduce(w[b] * a, axis=1) & (W - 1); c = look(v[..., None], np.arange(P))
                off = np.add.reduce(np.abs(pick(x[b], c.reshape(8, -1)).reshape(8, 16, Q, P) - a[..., None]), axis=1)
                best = np.take_along_axis(c, np.argmin(off, axis=-1)[..., None], -1)
                found[q][:, cut] = np.min(off, axis=-1) < t[b][:, 1:]
                fill[q][:, :, cut] = pick(x[b], ((best + 1 + np.arange(F)) & (W - 1)).reshape(8, -1)).reshape(8, 16, Q, F)
        found = found & live
        more = np.zeros((N, 8, W), np.int64); np.put_along_axis(more, site, found.astype(np.int64) * F, -1)
        place = here + np.add.accumulate(more, axis=-1) - more
        z = np.zeros((N, 8, 16, W + F * CAP + 1), np.int64)
        np.put_along_axis(z, place[:, :, None], pick(x, s), -1)
        at = np.take_along_axis(place, site, -1)[..., None] + 1 + np.arange(F)
        at = np.where(found[..., None], at, W + F * CAP).reshape(N, 8, 1, CAP * F)
        np.put_along_axis(z, at, fill.reshape(N, 8, 16, CAP * F), -1)
        x = np.ascontiguousarray(z[..., :W])
    return {"y": x.reshape(N, 128, W).astype(np.float32).astype(BF)}

from concourse.bass import DstId, RemoteDMATransfer
from concourse.mybir import AluOpType as Op, ActivationFunctionType as AF

NR, W, F, RO = 8, 2048, 4, 2
ND = NR - 1
NS = ND * 16
XW = 3072
NONE = 2064
DUMP = 2560
SL = 3
ENG = 2

SB = {
    "X0": (XW, "bfloat16"), "X1": (XW, "bfloat16"), "X2": (XW, "bfloat16"), "XC": (2048, "bfloat16"), "wtb": (1, "bfloat16"), "thi": (2, "int32"),
    "t1f": (1, "float32"), "t2f": (1, "float32"), "ones": (2048, "bfloat16"),
    "B144": (144, "bfloat16"), "Z": (144, "bfloat16"), "WZ": (144, "bfloat16"), "Z16": (144, "bfloat16"), "BOm2": (128, "bfloat16"),
    "TriS": (128, "bfloat16"), "TriI": (128, "bfloat16"), "Id": (128, "bfloat16"), "NId": (128, "bfloat16"), "EZ": (2048, "bfloat16"),
    "M16": (256, "bfloat16"), "R16c": (128, "bfloat16"), "Rk": (128, "bfloat16"), "Rs": (128, "bfloat16"), "R64k": (64, "bfloat16"),
    "Rc": (128, "bfloat16"), "WM": (256, "bfloat16"), "MOFF": (112, "float32"), "PP": (128, "float32"), "S2048": (16, "float32"),
    "D640": (8, "float32"), "RSW": (256, "bfloat16"), "R1": (128, "bfloat16"), "R2": (128, "bfloat16"), "S128": (256, "float32"),
    "N112": (112, "float32"), "MB": (112, "bfloat16"), "MT": (112, "int32"), "IT": (128, "bfloat16"), "ITa": (128, "bfloat16"),
    "O16": (128, "float32"), "tw": (64, "int32"), "tq": (64, "int32"), "tr": (64, "int32"), "tb": (448, "int32"), "tc": (448, "float32"),
    "tl": (448, "float32"), "tk": (512, "float32"), "KTw": (64, "bfloat16"), "KT": (1024, "bfloat16"),
    "vI": (128, "int32"), "u": (128, "int32"), "h": (128, "int32"), "hb": (128, "bfloat16"), "KK": (1024, "float32"),
    "QI": (1024, "int32"), "OI": (1024, "int32"), "OF": (1024, "uint16"), "G7": (2048, "bfloat16"), "G6": (2048, "bfloat16"),
    "E": (1024, "bfloat16"), "HS": (1024, "bfloat16"), "K3": (128, "float32"), "q3": (128, "int32"), "c3": (128, "int32"),
    "dp": (128, "float32"), "cc": (128, "float32"), "DV": (128, "float32"), "D2": (128, "float32"), "c10": (128, "float32"),
    "h5": (128, "float32"), "TF": (128, "float16"),
    "NX": (2064, "float32"), "GM": (256, "float16"), "CH": (256, "float16"), "LS": (128, "uint16"),
    "SA": (128, "float32"), "XS": (2048, "bfloat16"), "dI": (128, "int32"), "dA": (128, "int32"), "D1": (128, "bfloat16"),
    "CT": (128, "bfloat16"), "CQ": (128, "bfloat16"), "zz": (16, "float32"), "zs": (16, "float32"), "XB": (24, "float32"), "bs": (16, "float32"),
    "ps": (16, "float32"), "pl": (16, "uint16"), "VAL": (256, "float32"), "SW": (2304, "float32"), "nm": (112, "float32"),
    "YB": (224, "float32"), "YM": (224, "float32"), "YC": (224, "float32"), "VI": (112, "int32"), "PL": (112, "int32"),
    "wi": (16, "int32"), "wq": (8, "int32"), "wr": (8, "float32"), "wx": (8, "float32"), "kl": (8, "uint16"),
    "PR": (112, "float32"), "PM": (112, "float16"), "PC": (112, "float16"), "sl": (8, "uint16"), "P4": (8, "float32"), "nl": (112, "float32"),
    "aI": (8, "int32"), "U16": (112, "int32"), "H16": (112, "int32"), "K16": (112, "int32"), "Q16": (112, "int32"), "C16": (112, "int32"),
    "OA": (112, "uint16"), "A4": (448, "bfloat16"), "DA": (1792, "bfloat16"),
    "k1": (56, "float32"), "k2": (56, "float32"), "k3": (32, "float32"), "k4": (16, "float32"), "kb": (8, "float32"),
    "bi": (8, "int32"), "bm": (8, "int32"), "b2": (8, "float32"), "b3": (8, "float32"), "b4": (8, "int32"), "b5": (8, "int32"), "nf": (8, "float32"),
    "cf": (8, "float32"), "OL": (32, "uint16"),
    "FM": (112, "bfloat16"), "FC": (112, "bfloat16"), "X7": (8, "float32"), "in7": (8, "float32"), "A7": (8, "float32"), "zf": (8, "float32"),
    "zd": (8, "float32"), "AQ": (8, "float32"), "Ai": (8, "int32"), "lh": (16, "int32"), "lf": (16, "float32"), "hh": (8, "float32"),
    "SL": (32, "uint16"), "LD": (896, "bfloat16"), "RG": (896, "bfloat16"), "RE": (896, "bfloat16"), "SR": (128, "uint16"),
}
HOME = {}


def _pack():
    homes, n = {}, {}
    for k, (c, d) in SB.items():
        if c > 448 or k in ("wtb", "thi"):
            homes[k] = (c, d)
            HOME[k] = (k, 0)
        else:
            h = "pool_" + d
            o = n.get(h, 0)
            HOME[k] = (h, o)
            n[h] = o + (c + 15) // 16 * 16
            homes[h] = (n[h], d)
    return homes


SCRATCH = {k: ("sbuf", [128, c], d) for k, (c, d) in _pack().items()}
for _i in range(8):
    SCRATCH["D%d_" % _i] = ("sbuf", [128, 2048], "bfloat16")
    HOME["D%d_" % _i] = ("D%d_" % _i, 0)
    SCRATCH["p%d" % _i] = ("psum", [128, 512], "float32")
    HOME["p%d" % _i] = ("p%d" % _i, 0)
for _i in range(RO):
    for _n, _c in (("AS", 112), ("AL", 112), ("FS", 448), ("FL", 448)):
        SCRATCH["%s%d" % (_n, _i)] = ("sbuf", [128, _c], "bfloat16")
        HOME["%s%d" % (_n, _i)] = ("%s%d" % (_n, _i), 0)
SEMAPHORES = ["qV", "qS", "qP", "qG", "dX", "dW", "dT", "dY"] + ["%s%d" % (n, i) for i in range(RO) for n in ("ask", "ans", "la", "lb")]


def rank_program(g, core, T, topo):
    rank = T.rank_of(core)
    if rank is None:
        return
    queues = {"V": g.vector, "S": g.scalar, "P": g.tensor, "G": g, "Y": g.sync}
    done = {q: 0 for q in queues}
    known = {q: {} for q in queues}
    clocks, log = {}, {}

    def A(name, lo=0, hi=None, st=1, parts=128):
        home, o = HOME[name]
        if hi is None:
            hi = SB[name][0] if name in SB else SCRATCH[name][1][1]
        ap = T[home][0:parts, o + lo:o + hi] if st == 1 else T[home][0:parts, o + lo:o + hi:st]
        return (ap, [(home, o + lo, o + hi, st)])

    def I(win, off):
        return (win[0].indirect(off[0]), win[1] + off[1])

    def apart(lo, hi, st, lo2, hi2, st2):
        return lo >= hi2 or lo2 >= hi or (st == st2 and st > 1 and (lo - lo2) % st != 0)

    def sync(q, outs, ins):
        need = {}
        for w, regs in ((True, outs), (False, ins)):
            for (n, lo, hi, st) in regs:
                bank = n[0] == "p" and n[1].isdigit()
                for (q2, i2, lo2, hi2, st2, w2) in log.get(n, ()):
                    if bank and q2 != q:
                        hit = True
                    elif q2 == q and q == "P":
                        hit = False
                    else:
                        hit = (w or w2) and not apart(lo, hi, st, lo2, hi2, st2)
                    if hit:
                        need[q2] = max(need.get(q2, 0), i2)
        k = known[q]
        for q2, i2 in sorted(need.items(), key=lambda t: -sum(clocks[t].values())):
            if k.get(q2, 0) >= i2:
                continue
            queues[q].wait_ge(T.sem[q2 if q2 not in queues else "q" + q2], i2)
            for a, b in clocks[(q2, i2)].items():
                k[a] = max(k.get(a, 0), b)

    def note(q, i, outs, ins):
        for w, regs in ((True, outs), (False, ins)):
            for (n, lo, hi, st) in regs:
                def inside(e):
                    return lo <= e[2] and e[3] <= hi and (st == 1 or (e[4] == st and (e[2] - lo) % st == 0))
                l = log.setdefault(n, [])
                if w:
                    l[:] = [e for e in l if not (inside(e) and e[1] <= clocks[(q, i)].get(e[0], 0))]
                l[:] = [e for e in l if not (e[0] == q and e[5] == w and inside(e))]
                l.append((q, i, lo, hi, st, w))

    def do(q, call, outs, ins):
        o = [r for x in outs for r in x[1]]
        n = [r for x in ins for r in x[1]]
        sync(q, o, n)
        done[q] += 1
        call().then_inc(T.sem["q" + q], 1)
        c = dict(known[q])
        c[q] = done[q]
        clocks[(q, done[q])] = c
        note(q, done[q], o, n)

    def event(sem, val, outs, ins, base):
        c = dict(base)
        c[sem] = val
        clocks[(sem, val)] = c
        note(sem, val, [r for x in outs for r in x[1]], [r for x in ins for r in x[1]])

    def load(q, sem, out, src):
        queues[q].dma_start(out[0], src).then_inc(T.sem[sem], 16)
        event(sem, 16, [out], [], known[q])

    def cp(out, in_):
        do("V", lambda: g.vector.tensor_copy(out[0], in_[0]), [out], [in_])

    def tt(out, a, b, op):
        do("V", lambda: g.vector.tensor_tensor(out[0], a[0], b[0], op), [out], [a, b])

    def ts(out, a, s1, op0, s2=None, op1=None):
        col = isinstance(s1, tuple)
        x1 = s1[0] if col else s1
        ins = [a, s1] if col else [a]
        if op1 is None:
            do("V", lambda: g.vector.tensor_scalar(out[0], a[0], x1, None, op0), [out], ins)
        else:
            do("V", lambda: g.vector.tensor_scalar(out[0], a[0], x1, s2, op0, op1), [out], ins)

    def scan(out, a, b, op0=Op.mult, op1=Op.add):
        do("V", lambda: g.vector.tensor_tensor_scan(out[0], a[0], b[0], 0.0, op0, op1), [out], [a, b])

    def fill(out, c):
        do("V", lambda: g.vector.memset(out[0], c), [out], [])

    def act(out, in_, f=AF.Copy, **kw):
        ins = [in_] + [x for x in kw.values() if isinstance(x, tuple)]
        k2 = {a: x[0] if isinstance(x, tuple) else x for a, x in kw.items()}
        do("S", lambda: g.scalar.activation(out[0], in_[0], f, **k2), [out], ins)

    def mm(out, l, r, start=True, stop=True):
        do("P", lambda: g.tensor.matmul(out[0], l[0], r[0], start, stop), [out], [l, r])

    def sel(out, in_, pat, op, base, cm):
        do("G", lambda: g.affine_select(out[0], in_[0], pat, op, 0.0, base, cm), [out], [in_])

    def iota(out, pat, base, cm):
        do("G", lambda: g.iota(out[0], pat, base, cm, allow_small_or_imprecise_dtypes=True), [out], [])

    def Z(name, i):
        return A(name, 15 - i, 143 - i)

    def EZ(i):
        return A("EZ", 128 * i, 128 * i + 128)

    BO = A("B144", 0, 128)
    L16 = A("M16", 0, 128, parts=16)
    WP = A("p7", 384, 384 + NS)
    TH = A("p7", 256, 256 + NS)

    load("Y", "dX", A("X0", 0, W), T.x0[:])
    load("S", "dW", A("wtb"), T.wt[:])
    load("S", "dT", A("thi"), T.th[:])
    fill(A("ones", 0, 256), 1.0)
    fill(A("ones", 256, 2048), 1.0)
    iota(A("R64k", parts=16), [[0, 64]], 0, 64)
    iota(A("Rc"), [[1, 128]], 0, 0)
    sel(A("M16", parts=16), A("ones", 0, 256, parts=16), [[0, 16], [1, 16]], Op.is_equal, 0, -1)
    sel(A("B144"), A("ones", 0, 144), [[-16, 9], [0, 16]], Op.is_ge, 0, 1)
    sel(A("B144"), A("B144"), [[16, 9], [0, 16]], Op.is_ge, 15, -1)
    sel(A("Z"), A("B144"), [[0, 9], [1, 16]], Op.is_equal, -15, 0)
    sel(A("Id"), A("ones", 0, 128), [[-1, 128]], Op.is_equal, 0, 1)
    iota(A("R16c", parts=16), [[16, 128]], 0, 0)
    iota(A("Rk", parts=16), [[0, 128]], 0, 1)
    iota(A("Rs", parts=16), [[0, 128]], -2 * NS, 1)
    sel(A("EZ"), A("ones"), [[-1, 16], [-16, 8], [0, 16]], Op.is_equal, 0, 1)
    sel(A("RSW"), A("ones", 0, 256), [[0, 16], [1, 16]], Op.is_gt, 0, 0)
    sel(A("R1"), A("ones", 0, 128), [[0, 16], [1, 8]], Op.not_equal, -1, 0)
    sel(A("TriS"), BO, [[1, 128]], Op.is_gt, 0, -1)
    sel(A("TriI"), BO, [[1, 128]], Op.is_ge, 0, -1)
    iota(A("S128"), [[128, 256]], 128, 0)
    iota(A("N112"), [[1, 112]], 0, 0)
    iota(A("MB"), [[1, 16], [0, 7]], 0, 0)
    iota(A("MT"), [[2, 16], [0, 7]], 1, 0)
    iota(A("ITa"), [[0, 8], [1, 16]], 1, 0)
    fill(A("X0", W, W + 32), -1.0)
    fill(A("tk", 0, 64), -8.0)
    fill(A("E"), 0.0)
    fill(A("D1"), 0.0)
    fill(A("XB"), 0.0)
    fill(A("X7"), 0.0)
    mm(A("p7", 0, 256), L16, A("M16", parts=16))
    mm(A("p5", 0, 64), L16, A("R64k", parts=16), True, False)
    mm(A("p5", 0, 64), L16, A("Rc", 0, 64, parts=16), False, True)
    cp(A("tw"), A("p5", 0, 64))

    def part(name, k):
        return A(name, 64 * k, 64 * k + 64)

    ts(A("tq"), A("tw"), 127, Op.bitwise_and)
    ts(A("tr"), A("tw"), 7, Op.logical_shift_right)
    for k in range(7):
        ts(part("tb", k), A("tq"), 6 - k, Op.logical_shift_right, 1, Op.bitwise_and)
    cp(part("tc", 0), part("tb", 0))
    for k in range(1, 7):
        tt(part("tc", k), part("tc", k - 1), part("tb", k), Op.add)
    ts(A("WZ"), A("Z"), A("wtb"), Op.mult)
    cp(A("t1f"), A("thi", 0, 1))
    ts(A("t2f"), A("thi", 1, 2), 16.0, Op.mult)
    for k in range(7):
        tt(part("tl", k), part("tc", k), A("tr"), Op.is_le)
    for k in range(7):
        tt(A("KTw") if k == 6 else part("tk", k + 1), part("tk", k), part("tl", k), Op.add)

    def constants_1():
        mm(A("p6", 0, 128), L16, A("R16c", parts=16), True, False)
        mm(A("p6", 0, 128), L16, A("Rk", parts=16), False, True)
        act(A("PP"), A("p6", 0, 128))
        act(A("Z16"), A("Z"), scale=16.0)
        act(A("BOm2"), BO, scale=-2.0)
        act(A("R2"), A("R1"), scale=2.0)
        act(A("MOFF"), A("WM", 0, NS), scale=-1000.0, bias=1000.0)
        act(A("S2048"), A("PP", 0, 16), bias=2048.0)
        act(A("D640", 0, 7), A("PP", 0, 7), bias=float(DUMP // 4))
        act(A("SA", 0, 128, 8), A("PP", 0, 16), scale=8.0)

    def constants_2():
        cp(WP, A("WM", 0, NS))
        tt(A("O16"), A("ITa"), BO, Op.mult)
        ts(A("IT"), A("O16"), 1.0, Op.subtract)

    def table():
        for i in range(16):
            mm(A("p%d" % (4 + i // 8), 64 * (i % 8), 64 * (i % 8) + 64), EZ(i), A("KTw"))
        for b in range(2):
            act(A("KT", 512 * b, 512 * b + 512), A("p%d" % (4 + b)))

    def exchange(src, dst, w, ls, rs, back):
        sync("G", [], A(src)[1])
        tr = []
        for d in range(1, NR):
            to = T.cores[(rank - d) % NR if back else (rank + d) % NR]
            rid, pid, _ = topo.addr(to)
            mask = 0
            for e in topo.engines(core, to)[ENG * (d - 1):ENG * d]:
                mask |= 1 << e
            tr.append(RemoteDMATransfer(dst_ids=[DstId(rid=rid, pnc=pid)], dma_engine_mask=mask, remote_sem=T.sem[rs],
                                        src=A(src, w * (d - 1), w * d)[0], dst=A(dst, w * (d - 1), w * d)[0]))
        g.remote_dma_fused(tr, local_sem=T.sem[ls])
        event(rs, ENG * ND, [A(dst)], [], {})

    def one_round(rnd):
        X, XN = "X%d" % rnd, "X%d" % (rnd + 1)
        AL, AS, FL, FS = ("%s%d" % (n, rnd) for n in ("AL", "AS", "FL", "FS"))
        win = A(X, 0, W + 32)
        first = 7 - SL // 2

        def half(name, b):
            return A(name, 1024 * b, 1024 * b + 1024)

        for i in range(16):
            mm(A("p0", 0, 128), Z("WZ", i), A(X, i, W, 16), i == 0, i == 15)
        if rnd == 0:
            act(A("WM"), A("p7", 0, 256))
            act(A("NId"), A("Id"), scale=-1.0)
        for b in range(2):
            act(half("XC", b), half(X, b))
        cp(A("vI"), A("p0", 0, 128))
        ts(A("u"), A("vI"), 2047, Op.bitwise_and)
        ts(A("h"), A("u"), 5, Op.logical_shift_right)
        cp(A("hb"), A("h"))
        cp(A("p7", 0, 128), A("u"))

        def plus(m):
            act(A("KK", 128 * m, 128 * m + 128), A("hb"), bias=float(2 * m + 1))

        def look(m):
            return A("OI", 128 * m, 128 * m + 128)

        def prep(m0, m1):
            for m in range(m0, m1):
                tt(A("QI", 128 * m, 128 * m + 128), A("KK", 128 * m, 128 * m + 128), A("p7", 0, 128), Op.mult)
            ts(A("OI", 128 * m0, 128 * m1), A("QI", 128 * m0, 128 * m1), 2047, Op.bitwise_and)
            cp(A("OF", 128 * m0, 128 * m1), A("OI", 128 * m0, 128 * m1))

        def offs(m, b):
            return A("OF", 128 * m + 64 * b, 128 * m + 64 * b + 64)

        def pd(m, b=None):
            bank, o = (("p0", 0), ("p6", 0), ("p1", 0), ("p1", 1))[m] if m < 4 else ("p2", m - 4)
            return A(bank, 128 * o, 128 * o + 128) if b is None else A(bank, 128 * o + 64 * b, 128 * o + 64 * b + 64)

        def gather(m, b):
            tt(half("D%d_" % m, b), I(win, offs(m, b)), half("XC", b), Op.subtract)

        def absum(m, b):
            d = half("D%d_" % m, b)
            act(d, d, AF.Abs)
            sums(m, b)

        def sums(m, b):
            for i in range(16):
                mm(pd(m, b), Z("Z", i), A("D%d_" % m, 1024 * b + i, 1024 * b + 1024, 16), i == 0, i == 15)

        def near(m):
            ts(A("E", 8 - m, 1024, 8), pd(m), A("t1f"), Op.is_ge)

        order = [(m, b) for m in range(7, -1, -1) for b in range(2)]
        theirs = order[SL:]

        def own(m):
            bs = [b for b in range(2) if (m, b) in order[:SL]]
            for b in bs:
                act(half("G%d" % m, b), I(win, offs(m, b)))
                if (m, b) == (7, 0):
                    for x in range(first - 1, -1, -1):
                        plus(x)
            for b in bs:
                for x in (2 * b, 2 * b + 1):
                    mm(A("p%d" % (3 + x)), A("NId"), A(X, 512 * x, 512 * x + 512), True, False)
                    mm(A("p%d" % (3 + x)), A("Id"), A("G%d" % m, 512 * x, 512 * x + 512), False, True)
            for b in bs:
                for x in (2 * b, 2 * b + 1):
                    act(A("D%d_" % m, 512 * x, 512 * x + 512), A("p%d" % (3 + x)), AF.Abs)
                sums(m, b)

        for m in range(7, first - 1, -1):
            plus(m)
        prep(7, 8)
        own(7)
        prep(first, 7)
        for n, (m, b) in enumerate(theirs):
            gather(m, b)
            if n == 0:
                if rnd == 0:
                    constants_1()
                own(6)
                act(A("h5"), A("hb"), bias=5.0)
            if n == 1 - SL % 2:
                prep(0, first)
            if n:
                absum(*theirs[n - 1])
            if (m, b) == (3, 0) and rnd == 0:
                table()
            if (m, b) == (2, 1):
                if rnd == 0:
                    constants_2()
                for x in range(7, 3, -1):
                    near(x)
                fill(A("SW", 0, NS), 0.0)
        absum(*theirs[-1])

        tt(A("c10"), look(1), look(0), Op.subtract)
        near(3)
        near(2)
        scan(A("HS"), A("E"), A("E"))
        M = A("HS", 6, 1024, 8)
        T1, T2 = A("p7", 128, 256), A("p7", 256, 384)
        ts(T1, M, 2.0, Op.mult)
        ts(T2, M, 6.0, Op.is_ge)
        tt(A("K3"), T1, A("h5"), Op.add)
        tt(A("q3"), A("K3"), A("p7", 0, 128), Op.mult)
        ts(A("c3"), A("q3"), 2047, Op.bitwise_and)
        tt(A("dp"), A("PP"), A("c3"), Op.subtract)
        tt(A("cc"), A("c3"), look(1), Op.subtract)
        tt(T1, T2, A("dp"), Op.mult)
        tt(A("D2"), T1, A("cc"), Op.add)
        ts(A("p2", 256, 384), pd(1), A("t1f"), Op.is_ge)
        tt(A("p2", 384, 512), A("p2", 256, 384), A("D2"), Op.mult)
        tt(A("DV"), A("p2", 384, 512), A("c10"), Op.add)
        places = ((("p3", 0, 8, "V"), ("p4", 8, 16, "S")), (("p5", 0, 7, "S"), ("p6", 7, 13, "V"), ("p1", 13, 16, "S")))
        for b in range(2):
            lo, hi = 64 * b, 64 * b + 64
            e, d = A("p2", lo, hi), A("p2", 128 + lo, 128 + hi)
            ts(e, pd(0, b), A("t1f"), Op.is_ge)
            tt(d, e, A("DV", lo, hi), Op.mult)
            tt(A("TF", lo, hi), d, A("OI", lo, hi), Op.add)
            for p, i0, i1, q in places[b]:
                for i in range(i0, i1):
                    mm(A(p, 64 * (i - i0), 64 * (i - i0) + 64), EZ(i), A("TF", lo, hi))
        for b in range(2):
            for p, i0, i1, q in places[b]:
                for i in range(i0, i1):
                    o, n = A("NX", i + 1024 * b, 1024 * b + 1024, 16), A(p, 64 * (i - i0), 64 * (i - i0) + 64)
                    if q == "V":
                        ts(o, n, 1.0, Op.add)
                    else:
                        act(o, n, bias=1.0)
        cp(A("NX", W, W + 1), A("NX", 0, 1))
        cp(A(X, W, W + 4), A(X, 0, 4))

        act(A("XS", 0, W, 8), A(X, 0, W, 8))
        for k in range(1, 8):
            if k == 1:
                tt(A("GM"), A("NX", 0, W, 8), A("WM"), Op.mult)
            else:
                tt(A("GM"), I(A("NX", 0, W + 1), A("LS", 16 * k - 16, 16 * k)), A("WM"), Op.mult)
            scan(A("CH"), A("RSW"), A("GM"))
            cp(A("LS", 16 * k, 16 * k + 16), A("CH", 15, 256, 16))
            cp(A("SA", k, 128, 8), A("CH", 15, 256, 16))
            act(A("XS", k, W, 8), I(win, A("LS", 16 * k, 16 * k + 16)))

        tt(A("dI", 0, 127), A("SA", 1, 128), A("SA", 0, 127), Op.subtract)
        ts(A("dA", 0, 127), A("dI", 0, 127), 2047, Op.bitwise_and)
        ts(A("D1", 1, 128), A("dA", 0, 127), 1.0, Op.not_equal)
        scan(A("CT"), A("R1"), A("D1"))
        TW = A("CT", 7, 128, 8)
        mm(A("p7", 16, 32), BO, TW)
        mm(A("p7", 0, 16), A("TriS"), TW)
        scan(A("CQ"), A("R2"), A("D1"))
        for i in range(16):
            mm(A("p0", i, 256, 16), EZ(i), A("CQ", 7, 128, 8))
        ts(A("zz"), TW, 0.0, Op.is_equal)
        tt(A("zs"), A("zz"), A("S2048"), Op.mult)
        scan(A("XB", 1, 17), A("ones", 0, 16), A("p7", 16, 32))
        tt(A("bs"), A("p7", 0, 16), A("XB", 0, 16), Op.add)
        tt(A("ps"), A("bs"), A("zs"), Op.max)
        cp(A("pl"), A("ps"))
        tt(A("VAL"), A("p0", 0, 256), A("S128"), Op.add)
        cp(I(A("SW"), A("pl")), A("VAL"))
        scan(A("YB", 0, NS), A("SW", 0, NS), A("SW", 0, NS), Op.max, Op.max)
        ts(A("nm"), A("SW", 0, NS), 0.0, Op.is_equal)
        scan(A("YB", NS, 2 * NS), A("nm"), A("nm"))
        tt(A("YM", 0, NS), A("YB", 0, NS), WP, Op.mult)
        tt(A("YM", NS, 2 * NS), A("YB", NS, 2 * NS), WP, Op.mult)
        scan(A("YC"), A("RSW", 0, 2 * NS), A("YM"))
        cp(A("wi", 0, 7), A("YC", 15, NS, 16))
        ts(A("wr", 0, 7), A("YC", NS + 15, 2 * NS, 16), 7.0, Op.min, 128.0, Op.mult)
        ts(A("wq", 0, 7), A("wi", 0, 7), 127, Op.bitwise_and)
        tt(A("wx", 0, 7), A("wr", 0, 7), A("wq", 0, 7), Op.add)
        cp(A("kl", 0, 7), A("wx", 0, 7))
        cp(A("VI"), A("YB", 0, NS))
        ts(A("PL"), A("VI"), 4, Op.logical_shift_right, 65528, Op.bitwise_and)
        tt(A("PR"), I(A("KT"), A("kl", 0, 7)), A("PL"), Op.add)
        tt(A("PM"), A("PR"), WP, Op.mult)
        scan(A("PC"), A("RSW", 0, NS), A("PM"))
        cp(A("sl", 0, 7), A("PC", 15, NS, 16))
        cp(A(AS), I(A("XS"), A("sl", 0, 7)))
        exchange(AS, AL, 16, "la%d" % rnd, "ask%d" % rnd, False)
        ts(A("P4", 0, 7), A("PC", 15, NS, 16), 3.0, Op.subtract, 0.25, Op.mult)
        ts(A("nl"), A("N112"), A("XB", 16, 17), Op.is_ge, 1000.0, Op.mult)
        tt(TH, A("nl"), A("MOFF"), Op.max)

        for i in range(16):
            mm(A("p0", 0, 7), Z("WZ", i), A(AL, i, NS, 16), i == 0, i == 15)
        for b in range(4):
            act(A("A4", NS * b, NS * b + NS), A(AL))
        cp(A("aI", 0, 7), A("p0", 0, 7))
        ts(A("U16", 0, 7), A("aI", 0, 7), 2047, Op.bitwise_and)
        for n in (7, 14, 28, 56):
            cp(A("U16", n, 2 * n), A("U16", 0, n))
        ts(A("H16"), A("U16"), 5, Op.logical_shift_right)
        tt(A("K16"), A("H16"), A("MT"), Op.add)
        tt(A("Q16"), A("K16"), A("U16"), Op.mult)
        ts(A("C16"), A("Q16"), 2047, Op.bitwise_and)
        cp(A("OA"), A("C16"))

        def quarter(b):
            return A("DA", 448 * b, 448 * b + 448)

        act(A("G7", 0, 448), I(win, A("OA", 0, 28)))
        mm(A("p3", 0, 448), A("NId"), A("A4"), True, False)
        mm(A("p3", 0, 448), A("Id"), A("G7", 0, 448), False, True)
        for b in range(1, 4):
            tt(quarter(b), I(win, A("OA", 28 * b, 28 * b + 28)), A("A4"), Op.subtract)
            act(quarter(b), quarter(b), AF.Abs)
            if b == 1:
                act(quarter(0), A("p3", 0, 448), AF.Abs)
        for b in range(2):
            o = A("p%d" % (1 + b), 0, 56)
            mm(o, A("Id"), A("MB", 56 * b, 56 * b + 56), True, False)
            for i in range(16):
                mm(o, Z("Z16", i), A("DA", 896 * b + i, 896 * b + 896, 16), False, i == 15)
        cp(A("k1"), A("p1", 0, 56))
        tt(A("k2"), A("p2", 0, 56), A("k1"), Op.min)
        tt(A("k3", 0, 28), A("k2", 0, 28), A("k2", 28, 56), Op.min)
        tt(A("k4", 0, 14), A("k3", 0, 14), A("k3", 14, 28), Op.min)
        tt(A("kb", 0, 7), A("k4", 0, 7), A("k4", 7, 14), Op.min)
        cp(A("bi", 0, 7), A("kb", 0, 7))
        ts(A("nf", 0, 7), A("kb", 0, 7), A("t2f"), Op.is_ge, float(NONE - 1), Op.mult)
        ts(A("bm", 0, 7), A("bi", 0, 7), 15, Op.bitwise_and)
        ts(A("b2", 0, 7), A("bm", 0, 7), 2.0, Op.mult, 1.0, Op.add)
        tt(A("b3", 0, 7), A("b2", 0, 7), A("H16", 0, 7), Op.add)
        tt(A("b4", 0, 7), A("b3", 0, 7), A("U16", 0, 7), Op.mult)
        ts(A("b5", 0, 7), A("b4", 0, 7), 2047, Op.bitwise_and)
        tt(A("cf", 0, 7), A("b5", 0, 7), A("nf", 0, 7), Op.max)
        for f in (2, 3, 0, 1):
            ts(A("OL", 8 * f, 8 * f + 7), A("cf", 0, 7), float(1 + f), Op.add)
            if f > 1:
                act(A(FS, f, 448, F), I(win, A("OL", 8 * f, 8 * f + 7)))
        for f in (0, 1):
            cp(A(FS, f, 448, F), I(win, A("OL", 8 * f, 8 * f + 7)))
        exchange(FS, FL, 64, "lb%d" % rnd, "ans%d" % rnd, True)

        CN = A("p4", 0, 128)
        mm(CN, L16, A("R16c", parts=16), True, False)
        mm(CN, L16, A("Rs", parts=16), False, False)
        tt(A("FM"), A(FL, 0, 448, F), TH, Op.is_ge)
        scan(A("FC"), A("RSW", 0, NS), A("FM"))
        FW = A("FC", 15, NS, 16)
        mm(A("p7", 8, 15), BO, FW)
        mm(A("p7", 0, 7), A("TriI"), FW)
        ts(A("zf", 0, 7), FW, 0.0, Op.is_equal)
        tt(A("zd", 0, 7), A("zf", 0, 7), A("D640", 0, 7), Op.mult)
        scan(A("X7", 1, 8), A("ones", 0, 7), A("p7", 8, 15))
        tt(A("in7", 0, 7), A("p7", 0, 7), A("X7", 0, 7), Op.add)
        tt(A("A7", 0, 7), A("in7", 0, 7), A("P4", 0, 7), Op.add)
        tt(A("AQ", 0, 7), A("A7", 0, 7), A("zd", 0, 7), Op.max)
        ts(A("Ai", 0, 7), A("AQ", 0, 7), 4.0, Op.mult)
        ts(A("lh", 7, 14), A("Ai", 0, 7), 4, Op.logical_shift_right)
        ts(A("lh", 0, 7), A("Ai", 0, 7), 15, Op.bitwise_and)
        cp(A("lf", 0, 14), A("lh", 0, 14))
        ts(A("hh", 0, 7), A("lf", 7, 14), -1.0, Op.mult, -0.5, Op.add)
        for d in range(ND):
            rg, ld, re_ = (A(n, 128 * d, 128 * d + 128) for n in ("RG", "LD", "RE"))
            act(rg, A("Rc"), AF.Sign, bias=A("hh", d, d + 1))
            mm(CN, A("BOm2"), rg, False, False)
            ts(ld, A("IT"), A("lf", d, d + 1), Op.is_ge, -4.0, Op.mult)
            ts(re_, A("Rc"), A("lf", 7 + d, 8 + d), Op.is_equal)
            mm(CN, ld, re_, False, d == ND - 1)
        for f in range(F):
            ts(A("SL", 8 * f, 8 * f + 7), A("AQ", 0, 7), 4.0, Op.mult, float(f), Op.add)
        cp(A("SR"), CN)
        act(A(XN, 1024, 2048), I(A("XS"), A("SR", 64, 128)))
        cp(A(XN, 0, 1024), I(A("XS"), A("SR", 0, 64)))
        for f in range(F):
            cp(I(A(XN), A("SL", 8 * f, 8 * f + 7)), A(FL, f, 448, F))
        if rnd < RO - 1:
            fill(A(XN, W, W + 32), -1.0)

    for rnd in range(RO):
        one_round(rnd)

    y = A("X%d" % RO, 0, W)
    sync("Y", [], y[1])
    g.sync.dma_start(T.y[:], y[0]).then_inc(T.sem.dY, 16)
    g.sync.wait_ge(T.sem.dY, 16)
    for s in ("dX", "dW", "dT"):
        g.wait_ge(T.sem[s], 16)
    for q in ("V", "S", "P", "G"):
        g.wait_ge(T.sem["q" + q], done[q])
    for rnd in range(RO):
        for n in ("la", "lb", "ask", "ans"):
            g.wait_ge(T.sem["%s%d" % (n, rnd)], ENG * ND)
